import numpy as np, ml_dtypes
CORES = [48,51,52,55]
N = 4
BF = ml_dtypes.bfloat16
W, C, DH, S = 4096, 256, 512, 5
HI, LO, HA, HB = 10, 4, 1, 3
B, DB = W // C, DH // C
WT = np.array([37, 101, 59, 203, 83, 149, 11, 173, 67, 229, 127, 43, 191, 23, 251, 109])
def num(z):
    return np.sum(z * WT[:, None], axis=-2) & 4095
def place(u):
    return ((2741 * u) >> 5) & (DH - 1)
def pack(X, D, P, Q, z, l):
    a = np.ascontiguousarray
    return {"xr": a(X.reshape(N, 128, W)).astype(np.float32).astype(BF), "dr": a(D.reshape(N, 128, 2 * DH)).astype(np.int32),
            "pl": a(P.reshape(N, 128, C)).astype(np.int32), "ql": a(Q.reshape(N, 128, C)).astype(np.int32),
            "zq": a(z.reshape(N, 128, C)).astype(np.float32).astype(BF), "sd": a(l).astype(np.int32)}
def order(rng):
    return np.argsort(rng.random((8, W)), axis=1)
def over(pm):
    return np.broadcast_to(pm[None, :, None, :], (N, 8, 16, W))
def lay(pm, v):
    X = np.zeros((N, 8, 16, W), np.int64); np.put_along_axis(X, over(pm), v.astype(np.int64), 3)
    return X
def lanes(rng, pm, m):
    b = rng.integers(0, 16, (N, 8, 1, m)); t = rng.integers(0, W // 16, (N, 8, 16, m)); near = rng.random((N, 8, 1, m)) < 0.5
    return np.take_along_axis(over(pm), np.where(near, b * (W // 16) + t, rng.integers(0, W, (N, 8, 16, m))), 3)
def parts(rng):
    pm = order(rng)
    mid = np.repeat(rng.integers(60, 196, (N, 8, 16, 16)), W // 16, axis=3); amp = np.repeat(rng.choice(np.array([12.0, 40.0, 120.0]), (N, 8, 1, 16)), W // 16, axis=3)
    X = lay(pm, np.clip(np.floor(mid + amp * (2 * rng.random((N, 8, 16, W)) - 1)), 0, 255))
    return pm, X, lanes(rng, pm, 2 * DH), lanes(rng, pm, C), lanes(rng, pm, C), rng.integers(0, 256, (N, 8, 16, C)), rng.integers(0, 2, (N, 8, C))
def setup_inputs(rng):
    return pack(*parts(rng)[1:])
def setup_inputs_ends(rng):
    X = 255 * rng.integers(0, 2, (N, 8, 16, W)); dif = rng.choice(np.array([2, 3, 8, 16]), (N, 8)); dif[:, 7] = 16
    alt = np.argsort(rng.random((N, 8, 16)), axis=2) < dif[:, :, None]
    X[..., W - 1] = np.where(alt, 255 - X[..., 0], X[..., 0])
    cnt = rng.choice(np.array([0, LO - 1, LO, HI - 1, HI, 15, 16]), (N, 8, 1, 2 * DH))
    D = np.where(np.argsort(rng.random((N, 8, 16, 2 * DH)), axis=2) < cnt, W - 1, 0)
    kind = rng.integers(0, 3, (N, 8, 1, C)); Q = (W - 1) * np.where(kind == 2, rng.integers(0, 2, (N, 8, 16, C)), kind)
    P = (W - 1) * rng.integers(0, 2, (N, 8, 16, C)); l = rng.integers(0, 2, (N, 8, C))
    last = X[..., W - 1:]; half = np.argsort(rng.random((N, 8, 16, C)), axis=2) < 8; zk = rng.integers(0, 8, (N, 8, 1, C))
    z = 255 * rng.integers(0, 2, (N, 8, 16, C))
    z = np.where(zk == 0, 0, np.where(zk == 1, 255, np.where(zk == 2, 255 - last, np.where(zk == 3, X[..., :1], np.where(zk == 4, np.where(half, last, 255 - last), z)))))
    z[:, 7, :, C - 1] = 255 - X[:, 7, :, W - 1]; Q[:, 7, :, C - 1] = W - 1; l[:, 7, C - 1] = 1
    col = DH + place(num(z[:, 7, :, C - 1:]))[:, 0]
    for r in range(N): D[r, 7, :, col[r]] = W - 1
    return pack(X, D, P, Q, z, l)
def setup_inputs_corners(rng):
    pm = order(rng); V = W // 8; o = over(pm)
    b0 = rng.integers(2, 254, (N, 8, 16, 1)); b0[:, 1] = rng.integers(0, 3, (N, 16, 1)); b0[:, 6] = rng.integers(253, 256, (N, 16, 1))
    m = np.repeat(np.array([0, 0, 1, 2, 2, 3, 3, 4]), V)
    out = np.argsort(rng.random((N, 8, 16, W)), axis=2) < m
    by = 2 * rng.integers(0, 2, (N, 8, 16, W)) - 1; by = np.where(b0 == 0, 1, np.where(b0 == 255, -1, by))
    X = lay(pm, b0 + np.where(out, by, 0))
    cnt = rng.choice(np.array([0, LO - 1, LO, HI - 1, HI, 15, 16]), (N, 8, 1, 2 * DH)); odd = rng.random((N, 8, 1, 2 * DH)) < 0.35
    t = rng.integers(0, 2 * V, (N, 8, 16, 2 * DH)); t1 = t % V
    j = np.where(np.argsort(rng.random((N, 8, 16, 2 * DH)), axis=2) < cnt, np.where(odd, 2 * V + t1, 3 * V + t), np.where(odd, 3 * V + t1, 5 * V + t))
    D = np.take_along_axis(o, j, 3)
    own = B * np.arange(C) + rng.integers(0, B, (N, 8, 16, C)); ed = (W - 1) * rng.integers(0, 2, (N, 8, 16, C)); kind = rng.integers(0, 8, (N, 8, 1, C))
    Q = np.where(kind == 0, own, np.where(kind == 1, ed, np.take_along_axis(o, rng.integers(0, 2 * V, (N, 8, 16, C)), 3)))
    kind = rng.integers(0, 4, (N, 8, 1, C)); P = np.where(kind == 0, own, np.where(kind == 1, ed, np.take_along_axis(o, rng.integers(0, 8 * V, (N, 8, 16, C)), 3)))
    zk = rng.integers(0, 5, (N, 8, 1, C)); z = np.where(zk == 0, 0, np.where(zk == 1, 255, np.where(zk == 2, b0, rng.integers(0, 256, (N, 8, 16, C)))))
    l = (rng.random((N, 8, C)) < rng.choice(np.array([0.0, 0.5, 1.0]), (N, 8, 1))).astype(np.int64)
    return pack(X, D, P, Q, z, l)
def setup_inputs_crowd(rng):
    pm, X, D, P, Q, z, l = parts(rng)
    ix = np.zeros((8, C), np.int64)
    for g in (1, 3, 5, 7):
        e = C - 1 if g < 4 else int(rng.integers(1, C)); ix[g, e] = e
    w = np.broadcast_to(ix[None, :, None, :], (N, 8, 16, C))
    P, Q, z = [np.take_along_axis(v, w, 3) for v in (P, Q, z)]; l = np.take_along_axis(l, np.broadcast_to(ix[None], (N, 8, C)), 2)
    for v in (P, Q, z, l): v[1:, :2] = v[:1, :2]
    Q[:, 2:4] = Q[:, 2:4, :1].copy(); D[:, 2:4] = D[:, 2:4, :1].copy()
    D[:, 4:6] = Q[:, 4:6, :, :1]; D[:, 5, 15] = rng.integers(0, W, (N, 2 * DH))
    return pack(X, D, P, Q, z, l)
def setup_inputs_drops(rng):
    pm, X, D, P, Q, z, l = parts(rng); dg = (np.arange(8) % 3 != 2)[:, None, None]
    X1 = rng.integers(0, 101, X.shape); X1[..., W - 1] = 255
    Q1 = rng.integers(0, W - 1, Q.shape); z1 = rng.integers(0, 101, z.shape)
    if W == 4096:
        one = np.zeros((16, 1), np.int64); one[14] = 16; one[6] = 7
        pool = rng.integers(0, 101, (16, 32768)); pool = np.concatenate([one, pool[:, num(pool) >= 4064]], axis=1)
        high = np.argsort(rng.random((N, 8, 1, C)), axis=3) < C // 2
        z1 = np.where(high, np.moveaxis(pool[:, rng.integers(0, pool.shape[1], (N, 8, C))], 0, 2), z1)
        Q1 = np.where(high, rng.integers(W - 32, W - 1, Q.shape), Q1)
        z1[:, 7, :, C - 1] = one[:, 0]; Q1[:, 7, :, C - 1] = rng.integers(W - 32, W - 1, (N, 16)); Q1[:, 7, 15, C - 1] = 4075
    return pack(np.where(dg, X1, X), np.where(dg, W - 1, D), P, np.where(dg, Q1, Q), np.where(dg, z1, z), l)
def setup_inputs_spread(rng):
    e = rng.choice(np.array([1.0, 1.0, 3.0]), (N, 8, 1, 1))
    X = (np.exp2(8 * rng.random((N, 8, 1, W))) * rng.random((N, 8, 16, W))).astype(np.int64); z = (np.exp2(8 * rng.random((N, 8, 1, C))) * rng.random((N, 8, 16, C))).astype(np.int64)
    D, P, Q = [(W * rng.random((N, 8, 16, k)) ** e).astype(np.int64) for k in (2 * DH, C, C)]
    l = (rng.random((N, 8, C)) < rng.random((N, 8, 1))).astype(np.int64)
    return pack(X, D, P, Q, z, l)
def check_inputs(d):
    bad = []
    for k, lo, hi in (("xr", 0, 255), ("dr", 0, W - 1), ("pl", 0, W - 1), ("ql", 0, W - 1), ("zq", 0, 255), ("sd", 0, 1)):
        a = np.asarray(d[k]).astype(np.float64)
        if not (np.min(a) >= lo and np.max(a) <= hi): bad.append("range of " + k)
        elif np.any(a != np.floor(a)): bad.append("whole numbers in " + k)
    return bad
def go_on(v):
    h = C // 2
    return np.concatenate([np.roll(v[..., :h], HA, axis=0), np.roll(v[..., h:], HB, axis=0)], axis=-1)
def reference(xr, dr, pl, ql, zq, sd):
    X = xr.astype(np.float32).astype(np.int64).reshape(N, 8, 16, W); D = dr.astype(np.int64).reshape(N, 8, 16, 2 * DH)
    P = pl.astype(np.int64).reshape(N, 8, 16, C); Q = ql.astype(np.int64).reshape(N, 8, 16, C)
    z = zq.astype(np.float32).astype(np.int64).reshape(N, 8, 16, C); l = sd.astype(np.int64); A = np.zeros((N, 8, C), np.int64)
    c = np.arange(C); lane = np.arange(16)[:, None]
    for step in range(S):
        u = num(z)
        E = np.take_along_axis(D, (DH * l + place(u))[:, :, None, :], 3)
        x = np.take_along_axis(X, E.reshape(N, 8, 1, 16 * C), 3).reshape(N, 8, 16, 16, C)
        y = np.take_along_axis(X, Q.reshape(N, 8, 1, 16 * C), 3).reshape(N, 8, 16, 16, C)
        lo = np.min(y, axis=3); hi = np.max(y, axis=3)
        rows = np.sum((lo[:, :, :, None, :] <= x) & (x <= hi[:, :, :, None, :]), axis=2)
        ok = rows >= 14 + (A & 1)[:, :, None, :]; n = np.sum(ok, axis=2)
        dist = np.sum(np.abs(x - z[:, :, :, None, :]), axis=2)
        beta = np.argmin(np.where(ok, dist, 2 ** 20), axis=2)
        xb = np.take_along_axis(x, beta[:, :, None, None, :], 3)[:, :, :, 0, :]
        P1 = np.where(ok, E, P); made = (((Q * u[:, :, None, :]) >> 5) + Q + 37 * lane) & (W - 1)
        cont = (n >= HI)[:, :, None, :]; drop = (n < LO)[:, :, None, :]
        z = np.where(cont, np.abs(z - xb), np.where(drop, np.abs(z - hi), (z + xb) >> 1))
        u1 = num(z)
        dc = (DH * (1 - l) + DB * c + (u1 & (DB - 1)))[:, :, None, :]
        np.put_along_axis(D, dc, np.where(cont, P1, np.take_along_axis(D, dc, 3)), 3)
        xc = (B * c + (u1 & (B - 1)))[:, :, None, :]
        np.put_along_axis(X, xc, (np.take_along_axis(X, xc, 3) + z) >> 1, 3)
        P, Q = np.where(cont, P1, Q), np.where(cont, Q, np.where(drop, made, P1))
        l = np.where(n >= HI, l, 1 - l); A = A + (n < LO)
        if step < S - 1: P, Q, z, l, A = [go_on(v) for v in (P, Q, z, l, A)]
    return {"yx": X.reshape(N, 128, W).astype(np.float32).astype(BF), "yd": D.reshape(N, 128, 2 * DH).astype(np.float32), "yp": P.reshape(N, 128, C).astype(np.float32),
            "yq": Q.reshape(N, 128, C).astype(np.float32), "yz": z.reshape(N, 128, C).astype(np.float32).astype(BF), "ys": (2 * A + l).astype(np.float32)}

import numpy as np
from concourse.bass import DstId, RemoteDMATransfer
from concourse.mybir import AluOpType as A, ActivationFunctionType as F

S = 5
WT = (37, 101, 59, 203, 83, 149, 11, 173, 67, 229, 127, 43, 191, 23, 251, 109)
M2 = 25165824.0
LOW = -1000000.0

CFG = {
    "xeng": "vaaa", "yeng": "aaaa",
    "t2act": ((), ()),
    "wpe": False,
    "wide": False,
    "noise": 0.0, "seed": 0,
}


def sb(n, t):
    return ("sbuf", [128] + (list(n) if isinstance(n, tuple) else [n]), t)


f32, bf, i32, u16 = "float32", "bfloat16", "int32", "uint16"
SCRATCH = {
    "X": sb(4096, bf), "D": sb(2048, f32), "Di": sb(1024, i32), "Pi": sb(256, i32), "Qi": sb(256, i32),
    "zin": sb(256, bf), "sdi": sb(256, i32), "sdb": sb(256, bf),
    "PQi": sb(S * 512, f32), "PQo": sb(S * 512, f32), "Zi": sb(S * 256, bf), "Zo": sb(S * 256, bf),
    "Ui": sb(S * 256, u16), "Uo": sb(S * 256, u16), "Si": sb(S * 48, bf), "So": sb(S * 48, bf),
    "zh": sb(256, f32), "zn": sb(256, f32), "pie": sb(256, bf), "L": sb(64, u16),
    "Eu": sb(256, u16), "Ef": sb(256, f32), "dE": sb(256, f32), "tmp": sb(256, f32),
    "xg": sb(4096, bf), "yg": sb(4096, bf), "hs": sb(4096, bf), "ls": sb(4096, bf),
    "t1": sb((16, 16, 16), bf), "t2": sb((16, 16, 16), bf), "ab": sb((16, 16, 16), bf),
    "winQ": sb(1024, f32), "winZ": sb(1024, f32),
    "ma": sb(256, i32), "mb": sb(256, i32), "mc": sb(256, i32), "md": sb(256, i32), "Q37": sb(256, f32),
    "fail": sb(256, bf), "fT": sb(256, bf), "key": sb(256, f32), "best": sb(256, f32),
    "bi": sb(16, i32), "bj": sb(16, i32), "offw": sb(16, u16), "sel": sb(32, u16),
    "sg": sb(16, bf), "dl": sb(16, bf),
    "wg": sb(256, bf), "dd": sb(256, f32), "ri": sb(16, i32), "rj": sb(16, i32), "pm1": sb(16, i32),
    "Ib": sb(64, i32), "Cb": sb(32, f32), "Sb": sb(48, f32),
    "xa": sb(256, f32), "xe": sb(256, bf), "zo": sb(256, bf), "so": sb(16, f32), "sq": sb(16, bf), "yo": sb(256, f32),
    "iU": sb(4096, i32), "mH": sb(1024, bf), "mL": sb(1024, bf), "J": sb(160, f32), "JP": sb(160, f32),
    "pc": sb(8, i32), "pf": sb(8, f32), "wrow": sb(16, f32), "wm": sb(16, f32),
    "Id": sb(128, bf), "nI": sb(128, bf), "nhI": sb(128, bf), "n2I": sb(128, bf), "p2I": sb(128, bf), "hI": sb(128, bf),
    "S1": sb(144, bf), "Sh": sb(144, bf), "SK": sb(144, bf), "SW": sb(144, bf), "S8": sb(144, bf),
    "H0": sb(160, bf), "H1": sb(160, bf), "k1": sb(256, bf), "k2": sb(256, bf), "kf": sb(256, f32), "c8": sb(256, bf),
    "R": sb(256, f32), "half": sb(256, bf), "wa": sb(128, bf), "wb": sb(128, bf), "n512": sb(128, bf),
    "cl": sb(16, f32), "cs": sb(80, bf), "ti": sb(16, i32), "tl": sb(16, u16),
    "pL": ("psum", [128, 512], f32), "pH": ("psum", [128, 512], f32), "pA0": ("psum", [128, 512], f32),
    "pA1": ("psum", [128, 512], f32), "pO": ("psum", [128, 512], f32), "pK": ("psum", [128, 512], f32),
    "pM": ("psum", [128, 512], f32), "pV": ("psum", [128, 512], f32),
}
NDMA = 20
SEMAPHORES = (["ev", "ea", "ep", "eg", "sent"] + ["dm%d" % i for i in range(NDMA)]
              + ["ar%d" % i for i in range(4 * (S - 1))])


def build(g, core, T, topo, cfg):
    ops = []
    v, a, p = g.vector, g.scalar, g.tensor
    rank = T.rank_of(core)
    n = len(T.cores)

    def op(eng, kind, size, fn, r, w, bank=None, **kw):
        d = {"e": eng, "k": kind, "n": size, "f": fn, "r": list(r), "w": list(w), "b": bank}
        d.update(kw)
        ops.append(d)

    def ts(out, in0, s1, s2, o0, o1, r, w, size, kind="v1", bank=None):
        if o1 is None:
            op("v", kind, size, lambda: v.tensor_scalar(out, in0, s1, None, o0), r, w, bank)
        else:
            op("v", kind, size, lambda: v.tensor_scalar(out, in0, s1, s2, o0, o1), r, w, bank)

    def tt(out, in0, in1, o, r, w, size, kind="v2", bank=None):
        op("v", kind, size, lambda: v.tensor_tensor(out, in0, in1, o), r, w, bank)

    def cp(out, in_, r, w, size, kind="v1", bank=None):
        op("v", kind, size, lambda: v.tensor_copy(out, in_), r, w, bank)

    def ms(out, c, w, size, kind="v1", r=()):
        op("v", kind, size, lambda: v.memset(out, c), r, w)

    def scan(out, d0, d1, init, o0, o1, r, w, size, kind):
        op("v", kind, size, lambda: v.tensor_tensor_scan(out, d0, d1, init, o0, o1), r, w)

    def act(out, in_, func, r, w, size, kind="a1", bank=None, bias=0.0, scale=1.0):
        if func == F.Copy:
            op("a", kind, size, lambda: a.activation(out, in_, func), r, w, bank)
        else:
            op("a", kind, size, lambda: a.activation(out, in_, func, bias=bias, scale=scale), r, w, bank)

    def mm(groups, r, w, bank):
        def fn():
            last = None
            for out, cols, terms in groups:
                for i, (l, rh) in enumerate(terms):
                    last = p.matmul(out, l, rh, i == 0, i == len(terms) - 1)
            return last
        op("p", "pe", sum(max(64, c) * len(t) for o, c, t in groups), fn, r, w, bank,
           cnt=sum(len(t) for o, c, t in groups))

    def mmopen(out, cols, terms, start, stop, r, w, bank):
        def fn():
            last = None
            for i, (l, rh) in enumerate(terms):
                last = p.matmul(out, l, rh, start and i == 0, stop and i == len(terms) - 1)
            return last
        op("p", "pe", max(64, cols) * len(terms), fn, r, w, bank, cnt=len(terms))

    nd = [0]

    def dma(q, out, in_, r, w, nbytes):
        qq = g.sync if q == "s" else g.scalar
        sem = T.sem["dm%d" % nd[0]]
        nd[0] += 1
        op(q, "dma", nbytes, lambda: qq.dma_start(out, in_), r, w, sem=sem, inc=16)

    def iota(out, pat, base, cm, w, size, flt=True):
        if flt:
            op("g", "gp", size, lambda: g.iota(out, pat, base, cm, allow_small_or_imprecise_dtypes=True), [], w)
        else:
            op("g", "gp", size, lambda: g.iota(out, pat, base, cm), [], w)

    def gather(eng, out, win, off, r, w, size):
        if eng == "a":
            act(out, win.indirect(off), F.Copy, r, w, size, "ag")
        else:
            cp(out, win.indirect(off), r, w, size, "vg")

    def sel(Z, m):
        return Z[:, 15 - m:143 - m]

    dma("a", T.Qi[:], T.ql[:], [], ["Qi"], 1024)
    dma("s", T.X[:, 0:2048], T.xr[:, 0:2048], [], ["X0"], 4096)
    dma("a", T.zin[:], T.zq[:], [], ["zin"], 512)
    dma("s", T.X[:, 2048:4096], T.xr[:, 2048:4096], [], ["X1"], 4096)
    dma("a", T.sdi[0:8, :], T.sd[:], [], ["sdi"], 64)
    dma("s", T.Di[:], T.dr[:], [], ["Di"], 4096)
    dma("s", T.Pi[:], T.pl[:], [], ["Pi"], 1024)

    iota(T.pc[:, 0:1], [[0, 1]], 0, 1, ["pc0"], 1, False)
    iota(T.J[:], [[1, 160]], 0, 0, ["J"], 160)
    iota(T.JP[:], [[1, 160]], 0, -1, ["JP"], 160)
    iota(T.ti[:], [[1, 16]], 0, 0, ["ti"], 16, False)
    iota(T.kf[:], [[0, 16], [1, 16]], 0, 0, ["kf"], 256)
    iota(T.k2[:], [[256, 16], [0, 16]], 0, 0, ["k2r"], 256)
    iota(T.mH[:], [[0, 64], [256, 16]], 0, 0, ["mH"], 1024)
    iota(T.mL[:], [[0, 64], [-256, 16]], 256, 0, ["mL"], 1024)
    iota(T.iU[:], [[1, 4096]], 0, 0, ["iU"], 4096, False)
    ts(T.pc[:, 1:2], T.pc[:, 0:1], 15, None, A.bitwise_and, None, ["pc0"], ["pc1"], 1)
    ts(T.pc[:, 2:3], T.pc[:, 0:1], 112, None, A.bitwise_and, None, ["pc0"], ["pc2"], 1)
    ts(T.pc[:, 3:4], T.pc[:, 0:1], 16, None, A.bitwise_and, None, ["pc0"], ["pc3"], 1)
    cp(T.pf[:, 0:1], T.pc[:, 1:2], ["pc1"], ["pf0"], 1)
    ts(T.pf[:, 1:2], T.pc[:, 2:3], 15.0, None, A.add, None, ["pc2"], ["pf1"], 1)
    wr = ["wr%d" % i for i in range(16)]
    for i in range(16):
        ms(T.wrow[:, i:i + 1], WT[i] / 2.0, [wr[i]], 1)
    ts(T.wm[:], T.J[:, 0:16], T.pf[:, 0:1], None, A.is_equal, None, ["J", "pf0"], ["wm"], 16)
    tt(T.wm[:], T.wm[:], T.wrow[:], A.mult, ["wm"] + wr, ["wm"], 16)
    scan(T.wrow[:], T.wm[:], T.wm[:], 0.0, A.max, A.max, ["wm"], wr, 16, "v1")
    ts(T.pf[:, 3:4], T.pc[:, 1:2], 37.0, None, A.mult, None, ["pc1"], ["pf3"], 1)
    ts(T.pf[:, 4:5], T.pc[:, 3:4], 0.0, 0.5, A.is_equal, A.mult, ["pc3"], ["pf4"], 1)
    ts(T.pf[:, 5:6], T.pc[:, 3:4], 16.0, 0.5, A.is_equal, A.mult, ["pc3"], ["pf5"], 1)
    ts(T.pf[:, 6:7], T.pc[:, 1:2], 16.0, None, A.mult, None, ["pc1"], ["pf6"], 1)
    ts(T.pf[:, 7:8], T.pc[:, 0:1], 16.0, 15.0, A.mult, A.add, ["pc0"], ["pf7"], 1)
    ts(T.SW[:], T.J[:, 0:144], T.pf[:, 1:2], T.wrow[:, 15:16], A.is_equal, A.mult, ["J", "pf1", "wr15"], ["SW"], 144)
    ts(T.S8[:], T.J[:, 0:144], T.pf[:, 7:8], None, A.is_equal, None, ["J", "pf7"], ["S8"], 144)
    anyact = any(len(x) for x in cfg["t2act"])
    for nm, c in [("S1", 1.0), ("SK", 2.0 ** -12)] + ([("Sh", 0.5)] if anyact else []):
        ts(T[nm][:], T.J[:, 0:144], T.pf[:, 1:2], c, A.is_equal, A.mult, ["J", "pf1"], [nm], 144)
    ts(T.Id[:], T.JP[:, 0:128], 0.0, None, A.is_equal, None, ["JP"], ["Id"], 128)
    ids = [("nhI", -0.5), ("n2I", -2.0), ("nI", -1.0), ("wa", 0.078125), ("wb", -0.0390625), ("n512", -512.0)]
    ids += [("p2I", 2.0), ("hI", 0.5)] if cfg["wpe"] else []
    for nm, c in ids:
        act(T[nm][:], T.Id[:], F.Identity, ["Id"], [nm], 128, scale=c)
    ts(T.H0[:], T.JP[:], 16.0, T.pf[:, 4:5], A.is_equal, A.mult, ["JP", "pf4"], ["H0"], 160)
    ts(T.H1[:], T.JP[:], 16.0, T.pf[:, 5:6], A.is_equal, A.mult, ["JP", "pf5"], ["H1"], 160)
    act(T.key[:], T.kf[:], F.Identity, ["kf", "pf6"], ["key"], 256, bias=T.pf[:, 6:7])
    act(T.k1[:], T.key[:], F.Identity, ["key"], ["k1"], 256, scale=2.0 ** -24)
    act(T.k2[:], T.k2[:], F.Identity, ["k2r"], ["k2"], 256, scale=2.0 ** -24)
    ts(T.cl[:], T.ti[:], 16.0, T.pf[:, 0:1], A.mult, A.add, ["ti", "pf0"], ["cl"], 16)
    ts(T.tl[:], T.ti[:], 3.0, None, A.mult, None, ["ti"], ["tl"], 16)
    act(T.R[:], T.kf[:], F.Relu, ["kf"], ["R"], 256, bias=4.0, scale=-4.0)
    for i, (sc, bi) in enumerate(((4.0, 0.0), (16.0, 0.0), (2.0, 0.0), (0.0, 1.5), (0.0, 768.0))):
        act(T.cs[:, 16 * i:16 * i + 16], T.cl[:], F.Identity, ["cl"], ["cs%d" % i], 16, bias=bi, scale=sc)
    act(T.half[:], T.kf[:], F.Identity, ["kf"], ["half"], 256, bias=0.5, scale=0.0)
    act(T.winQ[:, 3:1024:4], T.kf[:], F.Copy, ["kf"], ["wQ3"], 256)
    act(T.winZ[:, 3:1024:4], T.kf[:], F.Copy, ["kf"], ["wZ3"], 256)
    if anyact:
        ms(T.c8[:], 0.0, ["c8"], 256, "vh")
        for h in range(2):
            for k0 in cfg["t2act"][h]:
                ms(T.c8[:, 128 * h + k0:128 * h + 128:2], 8.0, ["c8"], 64, "vh", ["c8"])

    def state(s, io):
        pq, z, u, sm = (T.PQi, T.Zi, T.Ui, T.Si) if io == "i" else (T.PQo, T.Zo, T.Uo, T.So)
        d = {"P": pq[:, 512 * s:512 * s + 256], "Q": pq[:, 512 * s + 256:512 * s + 512], "PQ": pq[:, 512 * s:512 * s + 512],
             "z2": z[:, 256 * s:256 * s + 256], "Qu": u[:, 256 * s:256 * s + 256], "sm": sm[:, 48 * s:48 * s + 48],
             "pi": sm[:, 48 * s:48 * s + 48:3], "mu": sm[:, 48 * s + 1:48 * s + 48:3], "A2": sm[:, 48 * s + 2:48 * s + 48:3]}
        d["z2m"] = [z[:, 256 * s + m:256 * s + 256:16] for m in range(16)]
        d["z2h"] = [z[:, 256 * s + 128 * h:256 * s + 128 * h + 128] for h in range(2)]
        d["z2j"] = [z[:, 256 * s + 64 * j:256 * s + 64 * j + 64] for j in range(4)]
        d["Quj"] = [u[:, 256 * s + 64 * j:256 * s + 64 * j + 64] for j in range(4)]
        d["Quh"] = [u[:, 256 * s + 128 * h:256 * s + 128 * h + 128] for h in range(2)]
        d["smh"] = [sm[:, 48 * s + 24 * h:48 * s + 24 * h + 24] for h in range(2)]
        d["PQh"] = [pq[:, 512 * s + 128 * j:512 * s + 128 * j + 128] for j in range(4)]
        d["t"] = lambda nm: "%s%s%d" % (nm, io, s)
        return d

    xc, dc, col, ul = T.L[:, 0:16], T.L[:, 16:32], T.L[:, 32:48], T.L[:, 48:64]

    m = state(0, "i")
    t = m["t"]
    cp(m["Qu"], T.Qi[:], ["Qi"], [t("Qu")], 256)
    act(m["z2"], T.zin[:], F.Identity, ["zin"], [t("z2")], 256, scale=2.0)
    cp(T.D[:, 0:1024], T.Di[:], ["Di"], ["D"], 1024)
    cp(T.sdb[0:8, :], T.sdi[0:8, :], ["sdi"], ["sdb"], 256)
    mm([(T.pV[:, 32:48], 16, [(T.S8[0:8, 15 - k:143 - k], T.sdb[0:8, k:256:16]) for k in range(16)])], ["S8", "sdb"], ["pW"], "pV")
    act(m["mu"], T.pV[:, 32:48], F.Identity, ["pW"], [t("mu")], 16, bank="pV", bias=-256.0, scale=512.0)
    cp(m["P"], T.Pi[:], ["Pi"], [t("P")], 256)
    cp(m["Q"], T.Qi[:], ["Qi"], [t("Q")], 256)
    ms(m["pi"], 1.0, [t("pi")], 16)
    ms(m["A2"], 0.0, [t("A2")], 16)

    nprep = [0]

    def prep_bank():
        nprep[0] += 1
        nm = "pA%d" % (nprep[0] % 2)
        return T[nm], nm

    def head(s):
        m = state(s, "i")
        t = m["t"]
        mm([(T.pV[:, 16:32], 16, [(sel(T.SW, k), m["z2m"][k]) for k in range(16)])], ["SW", t("z2")], ["pU"], "pV")
        cp(T.rj[:], T.pV[:, 16:32], ["pU"], ["rj"], 16, bank="pV")
        ts(T.Ib[:, 48:64], T.rj[:], 4095, None, A.bitwise_and, None, ["rj"], ["Ib3"], 16)
        ts(T.pm1[:], T.Ib[:, 48:64], 2741.0, None, A.mult, None, ["Ib3"], ["pm"], 16)
        ts(T.Ib[:, 32:48], T.pm1[:], 5, 511, A.arith_shift_right, A.bitwise_and, ["pm"], ["Ib2"], 16)
        tt(T.Sb[:, 32:48], T.Ib[:, 32:48], m["mu"], A.add, ["Ib2", t("mu")], ["Sb2"], 16)
        ts(col, T.Sb[:, 32:48], 256.0, None, A.add, None, ["Sb2"], ["col"], 16)
        cp(ul, T.Ib[:, 48:64], ["Ib3"], ["ul"], 16)
        Dw = T.D[:, 0:1024]
        cp(T.Eu[:], Dw.indirect(col), ["D", "col"], ["Eu"], 256, "vg")
        tt(T.dE[:], Dw.indirect(col), m["P"], A.subtract, ["D", "col", t("P")], ["dE"], 256, "vg")
        gather("a", T.Ef[:], Dw, col, ["D", "col"], ["Ef"], 256)
        gather("a", T.pie[:], m["sm"], T.tl[:], [t("pi"), t("mu"), t("A2"), "tl"], ["pie"], 256)
        if not cfg["wpe"]:
            act(T.zh[:], m["z2"], F.Identity, [t("z2")], ["zh"], 256, bias=-0.5, scale=0.5)
        for j in range(4):
            gather(cfg["yeng"][j], T.yg[:, 1024 * j:1024 * j + 1024], T.X[:], m["Quj"][j], ["X0", "X1", t("Qu")], ["y%d" % j], 1024)
        for j in range(4):
            gather(cfg["xeng"][j], T.xg[:, 1024 * j:1024 * j + 1024], T.X[:], T.Eu[:, 64 * j:64 * j + 64], ["X0", "X1", "Eu"], ["x%d" % j], 1024)
        act(T.pV[:, 256:512], m["Q"], F.Identity, [t("Q"), "pf3"], ["Q37"], 256, bank="pV", bias=T.pf[:, 3:4])
        act(T.winQ[:, 0:1024:4], m["Q"], F.Copy, [t("Q")], ["wQ0"], 256)
        tt(T.ma[:], T.iU[:].indirect(ul), m["Q"], A.mult, ["iU", "ul", t("Q")], ["ma"], 256, "vg")
        ts(T.mb[:], T.ma[:], 5, None, A.arith_shift_right, None, ["ma"], ["mb"], 256)
        tt(T.mc[:], T.mb[:], T.pV[:, 256:512], A.add, ["mb", "Q37"], ["mc"], 256, "v1", "pV")
        ts(T.md[:], T.mc[:], 4095, None, A.bitwise_and, None, ["mc"], ["md"], 256)
        cp(T.winQ[:, 2:1024:4], T.md[:], ["md"], ["wQ2"], 256)

    def passes(s, h):
        m = state(s, "i")
        t = m["t"]
        tb = slice(8 * h, 8 * h + 8)
        js = (2 * h, 2 * h + 1)
        ta = cfg["t2act"][h]
        for j in js:
            o = 1024 * j
            q, tq, xj = slice(o, o + 1024), slice(4 * j, 4 * j + 4), "x%d" % j
            scan(T.ls[:, q], T.mL[:], T.yg[:, q], 0.0, A.max, A.min, ["mL", "y%d" % j], ["ls%d" % j], 1024, "vh")
            scan(T.hs[:, q], T.mH[:], T.yg[:, q], 0.0, A.min, A.max, ["mH", "y%d" % j], ["hs%d" % j], 1024, "vh")
            lo, hi = T.ls[:, o + 15:o + 1024:16], T.hs[:, o + 15:o + 1024:16]
            mm([(T.pL[:, k:512:8], 64, [(T.Id[:], lo)]) for k in range(8)], ["Id", "ls%d" % j], ["pL"], "pL")
            if len(ta) < 2:
                mm([(T.pH[:, k:512:8], 64, [(T.Id[:], hi)]) for k in range(8)], ["Id", "hs%d" % j], ["pH"], "pH")

            def minus(lh, rh, e, r):
                bank, nm = prep_bank()
                if cfg["wide"]:
                    def fn():
                        p.matmul(bank[:], T.Id[:], T.xg[:, o + e:o + 1024:2], True, False)
                        for k in range(8):
                            last = p.matmul(bank[:, k:512:8], lh, rh, False, k == 7)
                        return last
                    op("p", "pe", 1024, fn, ["Id", xj] + r, [nm], nm, cnt=9)
                else:
                    mm([(bank[:, k:512:8], 64, [(T.Id[:], T.xg[:, o + 2 * k + e:o + 1024:16]), (lh, rh)]) for k in range(8)],
                       ["Id", xj] + r, [nm], nm)
                return bank, nm
            for e in range(2):
                bank, nm = minus(T.nhI[:], m["z2j"][j], e, ["nhI", t("z2")])
                act(T.ab[:, tq, :, e:16:2], bank[:], F.Abs, [nm], ["ab%d%d" % (j, e)], 512, bank=nm)
            for e in range(2):
                tt(T.t1[:, tq, :, e:16:2], T.xg[:, o + e:o + 1024:2], T.pL[:], A.is_lt, [xj, "pL"], ["t1%d%d" % (j, e)], 512, "v1", "pL")
            for e in range(2):
                if e in ta:
                    bank, nm = minus(T.nI[:], hi, e, ["nI", "hs%d" % j])
                    act(T.t2[:, tq, :, e:16:2], bank[:], F.Sign, [nm], ["t2%d%d" % (j, e)], 512, bank=nm, bias=-0.5)
                else:
                    tt(T.t2[:, tq, :, e:16:2], T.xg[:, o + e:o + 1024:2], T.pH[:], A.is_gt, [xj, "pH"], ["t2%d%d" % (j, e)], 512, "v1", "pH")
        if h == 1:
            mm([(T.pM[:, 256:512], 256, [(T.Id[:], m["z2"]), (T.n2I[:], T.hs[:, 15:4096:16])])],
               ["Id", "n2I", t("z2"), "hs0", "hs1", "hs2", "hs3"], ["pM1"], "pM")
            act(T.winZ[:, 2:1024:4], T.pM[:, 256:512], F.Abs, ["pM1"], ["wZ2"], 256, bank="pM")
        for e in range(2):
            ce = slice(128 * h + e, 128 * h + 128, 2)
            mm([(T.pK[:, ce], 64, [(T.Id[:], T.k1[:, ce]), (T.Id[:], T.k2[:, ce])]
                 + [(sel(T.SK, k), T.ab[:, tb, k, e:16:2]) for k in range(16)])],
               ["Id", "k1", "k2", "SK", "ab%d%d" % (js[0], e), "ab%d%d" % (js[1], e)], ["pK%d%d" % (h, e)], "pK")
        for e in range(2):
            ce = slice(128 * h + e, 128 * h + 128, 2)
            pre = [(T.nhI[:], T.pie[:, ce])]
            rd = ["nhI", "pie", "S1"]
            if ta:
                pre.append((T.Id[:], T.c8[:, ce]))
                rd += ["Id", "c8"]
            mmopen(T.pO[:, ce], 64, pre + [(sel(T.S1, k), T.t1[:, tb, k, e:16:2]) for k in range(16)], True, False,
                   rd + ["t1%d%d" % (j, e) for j in js], ["pO%d%d" % (h, e)], "pO")
            onact = e in ta
            mmopen(T.pO[:, ce], 64, [(sel(T.Sh if onact else T.S1, k), T.t2[:, tb, k, e:16:2]) for k in range(16)], False, True,
                   ["Sh" if onact else "S1"] + ["t2%d%d" % (j, e) for j in js], ["pO%d%d" % (h, e)], "pO")

    def travel(s, j, key, names, nb, after):
        mo, mi = state(s, "o"), state(s + 1, "i")
        sem = T.sem["ar%d" % (4 * s + j)]
        k = len(mo[key])
        trs, tot = [], 0
        for i in range(k):
            dst = T.cores[(rank + (1 if i % 2 == 0 else n - 1)) % n]
            rid, pid, se = topo.addr(dst)
            en = topo.engines(core, dst)
            q = len(en) // k
            trs.append(RemoteDMATransfer(dst_ids=[DstId(rid=rid, pnc=pid)], dma_engine_mask=sum(1 << x for x in en[q * i:q * i + q]),
                                         remote_sem=sem, src=mo[key][i], dst=mi[key][i]))
            tot += q
        tok = "fly%d%d" % (s, j)
        op("g", "send", nb, lambda: g.remote_dma_fused(trs, local_sem=T.sem.sent), [mo["t"](x) for x in names] + after, [tok, "g" + tok], cnt=tot)
        op("r", "recv", nb, None, [tok], [mi["t"](x) for x in names], sem=sem, inc=tot, rows=8 * k)
        return "g" + tok

    def tail(s):
        m, mo = state(s, "i"), state(s, "o")
        t, to = m["t"], mo["t"]
        last = s == S - 1
        e15 = slice(15, 256, 16)
        xs = ["x0", "x1", "x2", "x3"]
        he = ["00", "01", "10", "11"]
        ts(T.fail[:], T.pO[:, 0:256], 2.25, 2.0, A.is_ge, A.mult, ["pO" + x for x in he], ["fail"], 256, bank="pO")
        tt(T.key[:], T.pK[:, 0:256], T.fail[:], A.max, ["pK" + x for x in he] + ["fail"], ["key"], 256, "v1", "pK")
        scan(T.best[:], T.R[:], T.key[:], 0.0, A.add, A.min, ["R", "key"], ["best"], 256, "v1")
        ts(T.bi[:], T.best[:, e15], 2.0 ** 24, None, A.mult, None, ["best"], ["bi"], 16)
        ts(T.bj[:], T.bi[:], 4095, None, A.bitwise_and, None, ["bi"], ["bj"], 16)
        cp(T.offw[:], T.bj[:], ["bj"], ["offw"], 16)
        fk = [T.fail[:, k:256:16] for k in range(16)]
        mm([(T.pL[:, 16:32], 16, [(T.Id[:], T.cs[:, 0:16])] + [(T.wa[:], x) for x in fk]),
            (T.pL[:, 0:16], 16, [(T.Id[:], T.cs[:, 0:16]), (T.Id[:], T.cs[:, 48:64])] + [(T.wb[:], x) for x in fk])],
           ["Id", "cs0", "cs3", "wa", "wb", "fail"], ["pL"], "pL")
        selQ = T.sel[:, 16:32]
        ts(T.sel[:], T.pL[:, 0:32], -0.46875, None, A.add, None, ["pL"], ["selP", "selQ"], 32, bank="pL")
        mm([(T.pH[:, 32:48], 16, [(T.Id[:], x) for x in fk])], ["Id", "fail"], ["pH"], "pH")
        act(T.sg[:], T.pH[:, 32:48], F.Sign, ["pH"], ["sg"], 16, bank="pH", bias=13.0, scale=-1.0)
        act(T.dl[:], T.pH[:, 32:48], F.Sign, ["pH"], ["dl"], 16, bank="pH", bias=25.0, scale=-1.0)
        tt(mo["mu"], m["mu"], T.sg[:], A.mult, [t("mu"), "sg"], [to("mu")], 16)
        if not last:
            tt(mo["pi"], m["pi"], T.dl[:], A.mult, [t("pi"), "dl"], [to("pi")], 16)
        tt(mo["A2"], m["A2"], T.dl[:], A.add, [t("A2"), "dl"], [to("A2")], 16)
        mm([(T.pH[:, 0:16], 16, [(T.Id[:], T.cs[:, 16:32])]),
            (T.pH[:, 16:32], 16, [(T.Id[:], T.cs[:, 32:48]), (T.Id[:], T.cs[:, 64:80]), (T.nI[:], m["mu"]), (T.n512[:], T.sg[:])])],
           ["Id", "nI", "n512", "cs1", "cs2", "cs4", t("mu"), "sg"], ["pH"], "pH")
        op("v", "vh", 256, lambda: v.transpose(T.fT[:], T.fail[:]), ["fail"], ["fT"])
        gs = []
        for t2 in range(8):
            for s2 in range(2):
                Hs = T.H0 if s2 == 0 else T.H1
                gs.append((T.pM[:, 32 * t2 + 16 * s2:32 * t2 + 16 * s2 + 16], 16,
                           [(Hs[:, 16 - 16 * (h2 - s2):144 - 16 * (h2 - s2)],
                             T.fT[:, 32 * t2 + 16 * h2:32 * t2 + 16 * h2 + 16]) for h2 in range(2)]))
        mm(gs, ["H0", "H1", "fT"], ["pM0"], "pM")
        tt(T.pM[:, 0:256], T.pM[:, 0:256], T.dE[:], A.mult, ["pM0", "dE"], ["pM0"], 256, "v1", "pM")
        P1 = T.winQ[:, 1:1024:4]
        tt(P1, T.Ef[:], T.pM[:, 0:256], A.subtract, ["Ef", "pM0"], ["wQ1"], 256, "v1", "pM")
        wq = ["wQ0", "wQ1", "wQ2", "wQ3"]
        if not last:
            cp(mo["Qu"], T.winQ[:].indirect(selQ), wq + ["selQ"], [to("Qu")], 256, "vg")
        gather("a", mo["PQ"], T.winQ[:], T.sel[:], wq + ["selP", "selQ"], [to("P"), to("Q")], 512)
        z0, z1 = T.winZ[:, 0:1024:4], T.winZ[:, 1:1024:4]
        if cfg["wpe"]:
            gather("a", T.wg[:], T.xg[:], T.offw[:], xs + ["offw"], ["wg"], 256)
            bank, nm = prep_bank()
            mm([(bank[:, 0:256], 256, [(T.p2I[:], T.wg[:]), (T.nI[:], m["z2"])]),
                (bank[:, 256:512], 256, [(T.Id[:], T.wg[:]), (T.hI[:], m["z2"])])],
               ["p2I", "nI", "Id", "hI", "wg", t("z2")], [nm], nm)
            act(z0, bank[:, 0:256], F.Abs, [nm], ["wZ0"], 256, bank=nm)
            act(z1, bank[:, 256:512], F.Identity, [nm], ["wZ1"], 256, bank=nm, bias=-0.5)
        else:
            tt(T.dd[:], T.xg[:].indirect(T.offw[:]), T.zh[:], A.subtract, xs + ["offw", "zh"], ["dd"], 256, "vg")
            tt(z1, T.xg[:].indirect(T.offw[:]), T.zh[:], A.add, xs + ["offw", "zh"], ["wZ1"], 256, "vg")
            act(z0, T.dd[:], F.Abs, ["dd"], ["wZ0"], 256, bias=-1.0, scale=2.0)
        ts(mo["z2"], T.winZ[:].indirect(selQ), M2, M2, A.add, A.subtract, ["wZ0", "wZ1", "wZ2", "wZ3", "selQ"], [to("z2")], 256, "vg")
        mm([(T.pV[:, 0:16], 16, [(sel(T.SW, k), mo["z2m"][k]) for k in range(16)])], ["SW", to("z2")], ["pV"], "pV")
        act(T.zn[:], mo["z2"], F.Identity, [to("z2")], ["zn"], 256, bias=-0.5, scale=0.5)
        cp(T.ri[:], T.pV[:, 0:16], ["pV"], ["ri"], 16, bank="pV")
        ts(T.Ib[:, 0:16], T.ri[:], 15, None, A.bitwise_and, None, ["ri"], ["Ib0"], 16)
        ts(T.Ib[:, 16:32], T.ri[:], 1, None, A.bitwise_and, None, ["ri"], ["Ib1"], 16)
        tt(T.Sb[:, 0:32], T.Ib[:, 0:32], T.pH[:, 0:32], A.add, ["Ib0", "Ib1", "pH"], ["Sb0"], 32, "v1", "pH")
        cp(T.L[:, 0:32], T.Sb[:, 0:32], ["Sb0"], ["xc", "dc"], 32)
        tt(T.xa[:], T.X[:].indirect(xc), T.zn[:], A.add, ["X0", "X1", "xc", "zn"], ["xa"], 256, "vg")
        ts(T.xe[:], T.xa[:], M2, M2, A.add, A.subtract, ["xa"], ["xe"], 256)
        tt(T.X[:].indirect(xc), T.xe[:], T.half[:], A.mult, ["xe", "half", "xc"], ["X0", "X1"], 256, "vs")
        cp(T.D[:].indirect(dc), P1, ["wQ1", "dc"], ["D"], 256, "vs")
        if last:
            act(T.zo[:], mo["z2"], F.Identity, [to("z2")], ["zo"], 256, scale=0.5)
            ts(T.so[:], mo["mu"], 1.0 / 512, S + 0.5, A.mult, A.add, [to("mu")], ["so"], 16)
            tt(T.sq[:], T.so[:], mo["A2"], A.subtract, ["so", to("A2")], ["sq"], 16)
            mm([(T.pK[0:8, k:256:16], 16, [(T.Id[:, k:128:16], T.sq[:])]) for k in range(16)], ["Id", "sq"], ["pK" + x for x in he], "pK")
            act(T.yo[0:8, :], T.pK[0:8, 0:256], F.Copy, ["pK00"], ["yo"], 256, bank="pK")
            dma("s", T.yp[:], mo["P"], [to("P")], [], 1024)
            dma("s", T.yq[:], mo["Q"], [to("Q")], [], 1024)
            dma("s", T.yz[:], T.zo[:], ["zo"], [], 512)
            dma("s", T.ys[:], T.yo[0:8, :], ["yo"], [], 64)
            dma("s", T.yx[:, 0:2048], T.X[:, 0:2048], ["X0"], [], 8192)
            dma("a", T.yx[:, 2048:4096], T.X[:, 2048:4096], ["X1"], [], 8192)
            dma("s", T.yd[:], T.D[:, 0:1024], ["D"], [], 12288)
            return
        travel(s, 0, "Quh", ["Qu"], 256, [])
        travel(s, 1, "smh", ["pi", "mu", "A2"], 48, [])
        gz = travel(s, 2, "z2h", ["z2"], 256, [])
        travel(s, 3, "PQh", ["P", "Q"], 512, [gz])

    for s in range(S):
        head(s)
        passes(s, 0)
        passes(s, 1)
        tail(s)
    return ops


def depend(ops):
    writer, readers, bank = {}, {}, {}
    for i, o in enumerate(ops):
        hard, soft = set(), set()
        asyn = lambda j: ops[j]["k"] in ("dma", "recv", "send")
        for x in o["r"]:
            if x in writer:
                (soft if x.startswith("gfly") else hard).add(writer[x])
        for x in o["w"]:
            for j in readers.get(x, []) + ([writer[x]] if x in writer else []):
                if j != i:
                    (soft if ops[j]["e"] == o["e"] and not asyn(j) and not asyn(i) else hard).add(j)
        if o["b"]:
            e, cur, prev = bank.get(o["b"], (None, [], []))
            if e != o["e"]:
                prev, cur = cur, []
            hard.update(prev)
            if o["e"] == "p":
                soft.update(cur[-1:])
            bank[o["b"]] = (o["e"], cur + [i], prev)
        if o["e"] == "p":
            for j in list(hard):
                if ops[j]["e"] == "p":
                    hard.discard(j)
                    soft.add(j)
        for x in o["r"]:
            readers.setdefault(x, []).append(i)
        for x in o["w"]:
            writer[x] = i
            readers[x] = []
        o["hard"], o["soft"] = sorted(hard), sorted(soft - hard)


MODEL = {"g": 1.56, "s": 3.8, "fix": 50.0, "min": 50, "pe": 0.42, "pefix": 2.0, "same": 60.0, "cross": 120.0, "fly": 2000.0,
         "row": 50.0, "f": 1.2, "dma": 2000.0, "bw": 0.45, "send": 400.0, "peek": 100.0}


def cost(o, M):
    k, n, cy = o["k"], o["n"], 0.83 * M["f"]
    if k in ("v1", "vh", "v2", "a1"):
        return M["fix"] + max(M["min"], n * {"v1": 1, "vh": 0.5, "v2": 2, "a1": 1}[k]) * cy, 0.0
    if k in ("vg", "ag"):
        return M["fix"] + n * M["g"] * cy, 0.0
    if k == "vs":
        return M["fix"] + n * M["s"] * cy, 0.0
    if k == "pe":
        return (n * M["pe"] + o["cnt"] * M["pefix"]) * M["f"], 50.0
    if k == "gp":
        return 130 + 2 * n * cy, 0.0
    if k == "dma":
        return 100.0, M["dma"] + n * M["bw"]
    if k == "send":
        return M["send"], 0.0
    return 0.0, M["fly"] + o["rows"] * (M["row"] + n * 0.05)


def lag(ops, j, i, M):
    return M["same"] if ops[j]["e"] == ops[i]["e"] else M["cross"]


def plan(ops, M, noise, seed, bias):
    rng = np.random.RandomState(seed)
    n = len(ops)
    cs = [cost(o, M) for o in ops]
    succ = [[] for o in ops]
    for i, o in enumerate(ops):
        for j in o["hard"] + o["soft"]:
            succ[j].append(i)
    pr = [0.0] * n
    for i in range(n - 1, -1, -1):
        pr[i] = cs[i][0] + cs[i][1] + max([pr[k] + M["cross"] for k in succ[i]] + [0.0])
    pr = [x + noise * float(rng.randn()) + bias.get(o["e"] + (o["w"] or ["out"])[0], 0.0) for x, o in zip(pr, ops)]
    left = [len(o["hard"]) + len(o["soft"]) for o in ops]
    rdy = [0.0] * n
    free, order, cand = {}, {}, {}
    for i, o in enumerate(ops):
        free.setdefault(o["e"], 0.0)
        order.setdefault(o["e"], [])
        cand.setdefault(o["e"], [])
        if not left[i]:
            cand[o["e"]].append(i)
    end = 0.0
    for it in range(n):
        bst = None
        for e, cs_e in cand.items():
            if not cs_e:
                continue
            t0 = max(free[e], min(rdy[i] for i in cs_e))
            i = max((i for i in cs_e if rdy[i] <= t0 + M["peek"]), key=lambda i: pr[i])
            if bst is None or t0 < bst[0]:
                bst = (t0, max(free[e], rdy[i]), i, e)
        t0, st, i, e = bst
        cand[e].remove(i)
        order[e].append(i)
        if e != "r":
            free[e] = st + cs[i][0]
        done = st + cs[i][0] + cs[i][1]
        end = max(end, done)
        for k in succ[i]:
            rdy[k] = max(rdy[k], done + lag(ops, i, k, M) if i in ops[k]["hard"] else st)
            left[k] -= 1
            if not left[k]:
                cand[ops[k]["e"]].append(k)
    return order, end


def emit(g, T, ops, order):
    qs = {"v": g.vector, "a": g.scalar, "p": g.tensor, "g": g, "s": g.sync}
    sems = {"v": T.sem.ev, "a": T.sem.ea, "p": T.sem.ep, "g": T.sem.eg}
    pos = {}
    for e, l in order.items():
        for k, i in enumerate(l):
            pos[i] = k
    own = lambda o: "sem" in o
    seq, at, done = [], dict((e, 0) for e in order), set()
    while len(seq) < len(ops):
        for e, l in order.items():
            while at[e] < len(l) and all(j in done for j in ops[l[at[e]]]["hard"] + ops[l[at[e]]]["soft"]):
                seq.append(l[at[e]])
                done.add(l[at[e]])
                at[e] += 1
    know = dict((e, {}) for e in order)
    snap, waits, signal = {}, {}, set()
    for i in seq:
        o = ops[i]
        e = o["e"]
        if e == "r":
            snap[i] = {}
            continue
        kn = know[e]
        ws = []
        for j in sorted(o["hard"], key=lambda j: -pos[j]):
            key = ("d", j) if own(ops[j]) else ops[j]["e"]
            if kn.get(key, -1) >= pos[j]:
                continue
            ws.append(j)
            signal.add(j)
            kn[key] = pos[j]
            for k2, x in snap[j].items():
                if kn.get(k2, -1) < x:
                    kn[k2] = x
        waits[i] = ws
        snap[i] = dict(kn)
    count = dict((e, 0) for e in sems)
    val = {}
    for e in sems:
        for i in order[e]:
            if i in signal and not own(ops[i]):
                count[e] += 1
                val[i] = count[e]
    sent = 0
    for i in seq:
        o = ops[i]
        if o["e"] == "r":
            continue
        q = qs[o["e"]]
        for j in waits[i]:
            if own(ops[j]):
                q.wait_ge(ops[j]["sem"], ops[j]["inc"])
            else:
                q.wait_ge(sems[ops[j]["e"]], val[j])
        ins = o["f"]()
        if o["k"] == "send":
            sent += o["cnt"]
        elif own(o):
            ins.then_inc(o["sem"], o["inc"])
        elif i in val:
            ins.then_inc(sems[o["e"]], 1)
    if sent:
        g.wait_ge(T.sem.sent, sent)
    for i, o in enumerate(ops):
        if o["k"] == "dma" and i not in signal:
            g.sync.wait_ge(o["sem"], o["inc"])


ORDER = {}
BIAS = {'aab00': 6000, 'aab01': 6000, 'aab10': 6000, 'aab11': 4500, 'ppA0': 3000, 'ppA1': 3000, 'vmc': -3000, 'vhs3': 500,
        'vtl': 3000, 'ppO11': -500, 'aab21': 3000, 'acs1': -1500, 'ppK11': -500, 'vhs0': 6000, 'vt221': 500, 'vt210': -1500,
        'aQ37': 3000, 'vhs1': 1500, 'ak2': -500, 'ppL': 1500, 'vPi0': 500, 'ppO01': -1500, 'vt121': 6000, 'ayo': 6000,
        'vls3': -6000, 'vt101': -1500, 'vpc3': 6000, 'ahalf': 3000, 'aab20': 6000, 'akey': 1500, 'ax2': -500, 'vz2o1': -1500,
        'aEf': 7500, 'vt211': -1500, 'vdE': -500, 'asg': 6000, 'vkey': 500, 'vEu': 1500, 'vbi': -6000, 'aab31': 6000,
        'vIb1': -3000, 'vhs2': 6000, 'acs3': -6000, 'vbj': 4500, 'vpf4': 500, 'vxc': -500, 'vls0': 1500, 'aPo1': 3500,
        'ppU': -2000, 'vwQ1': -3000, 'awQ0': 500, 'awQ3': -6000, 'aout': 1500, 'vso': -500, 'vrj': 4500, 'vfT': -3000,
        'aR': -6000, 'vbest': 500, 'asdi': 500, 'vt111': -6000, 'vpm': 500, 'an512': -3000, 'vwQ2': 3000, 'vpM0': -1500,
        'vt100': -1500}


def rank_program(g, core, T, topo):
    if T.rank_of(core) is None:
        return
    ops = build(g, core, T, topo, CFG)
    depend(ops)
    if "o" not in ORDER:
        ORDER["o"] = plan(ops, MODEL, CFG["noise"], CFG["seed"], BIAS)[0]
    emit(g, T, ops, ORDER["o"])
